import numpy as np
import ml_dtypes


def mxq(x, axis, fmt="e4m3"):
    dtype, down = {"e4m3": (ml_dtypes.float8_e4m3fn, 7), "e5m2": (ml_dtypes.float8_e5m2, 14)}[fmt]
    v = np.moveaxis(np.asarray(x, np.float32).astype(ml_dtypes.bfloat16).astype(np.float64), axis, -1)
    blocks = v.reshape(v.shape[:-1] + (-1, 32))
    amax = np.abs(blocks).max(-1, keepdims=True)
    byte = np.maximum(np.where(amax > 0, np.frexp(amax)[1] - 1 + 127, 0) - down, 1)
    scale = np.exp2(byte - 127.0)
    codes = (blocks / scale).astype(np.float32).astype(dtype).astype(np.float64)
    return np.moveaxis((codes * scale).reshape(v.shape), -1, axis)


WIDE = False


def mx_kscale(k):
    if not WIDE:
        return np.ones(k)
    levels = np.array([10, -10, 5, -5, 0])
    if k % 512:
        return np.exp2(np.random.permutation(np.resize(levels, k // 32))).repeat(32)
    a = np.empty((k // 512, 16))
    for p in range(k // 512):
        a[p, :8] = np.random.permutation(np.resize(levels, 8))
        for g in range(8):
            far = levels[np.abs(levels - a[p, g]) >= 10]
            a[p, g + 8] = far[np.random.randint(len(far))]
    return np.exp2(a.ravel()).repeat(32)


def f64(x):
    return np.asarray(x).astype(np.float64)


def striped(idx):
    return np.tile(idx.reshape(-1, 16).T, (8, 1)).astype(np.uint16)


def unstriped(offs):
    return offs[:16].T.reshape(-1).astype(np.int64)


def relu(v):
    return np.maximum(v, 0.0)


K, T, D, S, V, N = 512, 1024, 4, 2048, 512, 256


def setup_inputs():
    n = np.random.standard_normal
    s = mx_kscale(K)[:, None]
    return {
        "xT": (n((K, T)) * s).astype(np.float32),
        "w": (n((K, N)) / np.sqrt(K) / s).astype(np.float32),
        "b": (0.3 * n((N, 1))).astype(np.float32),
        "gate": np.tile(np.random.uniform(0.2, 1.0, (D, 1, V)) / np.sqrt(D), (1, N, 1)).astype(np.float32),
        "pos1": striped(np.random.permutation(T)[:V]),
        "pos2": striped(np.random.permutation(T)[:V]),
        "pos3": striped(np.random.permutation(T)[:V]),
        "pos4": striped(np.random.permutation(T)[:V]),
    }


def reference(xT, w, b, gate, pos1, pos2, pos3, pos4):
    y = mxq(f64(w), 0, "e4m3").T @ mxq(f64(xT), 0, "e4m3")
    y = relu(y + f64(b))
    return sum(f64(gate[d]) * y[:, unstriped(p)] for d, p in enumerate((pos1, pos2, pos3, pos4)))

@@ -1,0 +1,132 @@
+from contextlib import ExitStack
+
+import concourse.mybir as mybir
+
+K, T, D, V, N = 512, 1024, 4, 512, 256
+P = 128
+J = 4
+X_CHUNKS = ((0, 512, 192), (512, 256, 96), (768, 256, 64))
+
+FLOPS = 2 * K * T * N + 2 * T * N + 2 * D * N * V
+
+F32 = mybir.dt.float32
+BF16 = mybir.dt.bfloat16
+U32 = mybir.dt.uint32
+U16 = mybir.dt.uint16
+U8 = mybir.dt.uint8
+FP8X4 = mybir.dt.float8_e4m3fn_x4
+RELU = mybir.ActivationFunctionType.Relu
+MULT = mybir.AluOpType.mult
+
+
+def tile_picked_agg_lin_relu_sub_l_kernel(tc, xT, w, b, gate, pos1, pos2, pos3, pos4, out):
+    nc = tc.nc
+    with ExitStack() as ctx:
+        keep = ctx.enter_context(tc.tile_pool(name="keep", bufs=1))
+        psum = ctx.enter_context(tc.psum_pool(name="psum", bufs=1))
+
+        w_rows = w.rearrange("(p j) m -> p j m", j=J)
+        x_rows = xT.rearrange("(p j) t -> p j t", j=J)
+
+        w_raw = [keep.tile([P, J, P], F32, name=f"w_raw{h}") for h in range(2)]
+        x_raw = [keep.tile([P, J, n], F32, name=f"x_raw{c}") for c, (t0, n, s) in enumerate(X_CHUNKS)]
+        bias = [keep.tile([P, 1], F32, name=f"bias{h}") for h in range(2)]
+        lists = [keep.tile([P, V // 16], U16, name=f"list{d}") for d in range(D)]
+        gates = [[keep.tile([P, V], F32, name=f"gate{d}_{h}") for d in range(D)] for h in range(2)]
+
+        warm = keep.tile([P, 1], F32, name="warm")
+        warmed = keep.tile([P, 1], F32, name="warmed")
+        nc.gpsimd.memset(warm[:], 0.0)
+        nc.scalar.activation(warmed[:], warm[:], RELU)
+
+        nc.sync.dma_start(out=w_raw[0][:], in_=w_rows[:, :, 0:P])
+        for c, (t0, n, s) in enumerate(X_CHUNKS):
+            nc.sync.dma_start(out=x_raw[c][:], in_=x_rows[:, :, t0 : t0 + n])
+        for h in range(2):
+            nc.scalar.dma_start(out=bias[h][:], in_=b[h * P : (h + 1) * P, :])
+        pos = (pos1, pos2, pos3, pos4)
+        nc.sync.dma_start(lists[0][:], pos[0])
+        nc.sync.dma_start(out=gates[0][0][:], in_=gate[0, 0:P, :])
+        nc.sync.dma_start(out=w_raw[1][:], in_=w_rows[:, :, P : 2 * P])
+        for d in range(1, D):
+            nc.sync.dma_start(lists[d][:], pos[d])
+            nc.sync.dma_start(out=gates[0][d][:], in_=gate[d, 0:P, :])
+        for d in range(D):
+            nc.sync.dma_start(out=gates[1][d][:], in_=gate[d, P : 2 * P, :])
+
+        w_grp = [keep.tile([P, P, J], BF16, name=f"w_grp{h}", align_bytes=64) for h in range(2)]
+        w_codes = [keep.tile([P, P], U32, name=f"w_codes{h}", align_bytes=64) for h in range(2)]
+        w_scales = [keep.tile([P, P], U8, name=f"w_scales{h}", align_bytes=64) for h in range(2)]
+        x_grp = [keep.tile([P, n, J], BF16, name=f"x_grp{c}", align_bytes=64) for c, (t0, n, s) in enumerate(X_CHUNKS)]
+        x_codes = [keep.tile([P, n], U32, name=f"x_codes{c}", align_bytes=64) for c, (t0, n, s) in enumerate(X_CHUNKS)]
+        x_scales = [keep.tile([P, n], U8, name=f"x_scales{c}", align_bytes=64) for c, (t0, n, s) in enumerate(X_CHUNKS)]
+        y = [keep.tile([P, T], F32, name=f"y{h}") for h in range(2)]
+
+        def quantise(codes, scales, grp):
+            nc.vector.quantize_mx(
+                out=codes[:].bitcast(FP8X4), scales=scales[:], in_=grp[:].rearrange("p w j -> p (w j)")
+            )
+
+        def project(h, c):
+            t0, n, s = X_CHUNKS[c]
+            acc = psum.tile([P, n], F32, name=f"acc{h}_{c}")
+            nc.tensor.matmul_mx(
+                out=acc[:],
+                lhsT=w_codes[h][:].bitcast(FP8X4),
+                lhsT_scale=w_scales[h][:],
+                rhs=x_codes[c][:].bitcast(FP8X4),
+                rhs_scale=x_scales[c][:],
+                start=True,
+                stop=True,
+            )
+            return acc
+
+        def activate(h, c, acc):
+            t0, n, s = X_CHUNKS[c]
+            nc.scalar.activation(y[h][:, t0 : t0 + n], acc[:], RELU, bias=bias[h][:])
+
+        nc.vector.tensor_copy(out=w_grp[0][:], in_=w_raw[0][:].rearrange("p j m -> p m j"))
+        quantise(w_codes[0], w_scales[0], w_grp[0])
+        for c, (t0, n, s) in enumerate(X_CHUNKS):
+            v = n - s
+            nc.scalar.copy(out=x_grp[c][:, v:n, :], in_=x_raw[c][:, :, v:n].rearrange("p j t -> p t j"))
+            nc.vector.tensor_copy(out=x_grp[c][:, 0:v, :], in_=x_raw[c][:, :, 0:v].rearrange("p j t -> p t j"))
+            quantise(x_codes[c], x_scales[c], x_grp[c])
+        for c in range(len(X_CHUNKS)):
+            activate(0, c, project(0, c))
+
+        nc.scalar.copy(out=w_grp[1][:], in_=w_raw[1][:].rearrange("p j m -> p m j"))
+
+        def fetch(h, d, v0, v1, product):
+            nc.vector.tensor_tensor(
+                product, y[h][:].indirect(lists[d][:, v0 // 16 : v1 // 16]), gates[h][d][:, v0:v1], MULT
+            )
+
+        pair = [keep.tile([P, 2, V], F32, name=f"pair{d}") for d in (0, 2)]
+        pair_sum = keep.tile([P, 2, V], F32, name="pair_sum")
+        prod = [keep.tile([P, V], F32, name=f"prod{d}") for d in range(D)]
+        s01 = keep.tile([P, V], F32, name="s01")
+        s012 = keep.tile([P, V], F32, name="s012")
+        total = [keep.tile([P, V], F32, name=f"total{h}") for h in range(2)]
+
+        fetch(0, 0, 0, V, pair[0][:, 0, :])
+        quantise(w_codes[1], w_scales[1], w_grp[1])
+        for c in range(len(X_CHUNKS)):
+            activate(1, c, project(1, c))
+        fetch(0, 1, 0, V, pair[0][:, 1, :])
+        fetch(0, 2, 0, V, pair[1][:, 0, :])
+        fetch(0, 3, 0, V, pair[1][:, 1, :])
+        fetch(1, 0, 0, V, prod[0][:])
+        nc.vector.tensor_add(pair_sum[:], pair[0][:], pair[1][:])
+        fetch(1, 1, 0, V, prod[1][:])
+        nc.vector.tensor_add(total[0][:], pair_sum[:, 0, :], pair_sum[:, 1, :])
+        nc.sync.dma_start(out=out[0:P, :], in_=total[0][:])
+        fetch(1, 2, 0, V, prod[2][:])
+        nc.vector.tensor_add(s01[:], prod[0][:], prod[1][:])
+        fetch(1, 3, 0, V // 2, prod[3][:, 0 : V // 2])
+        nc.vector.tensor_add(s012[:], s01[:], prod[2][:])
+        fetch(1, 3, V // 2, V, prod[3][:, V // 2 : V])
+        for v0 in (0, V // 2):
+            cols = slice(v0, v0 + V // 2)
+            nc.vector.tensor_add(total[1][:, cols], s012[:, cols], prod[3][:, cols])
+            nc.sync.dma_start(out=out[P : 2 * P, cols], in_=total[1][:, cols])

@@ -5,7 +5,10 @@ import concourse.mybir as mybir
 K, T, D, V, N = 512, 1024, 4, 512, 256
 P = 128
 J = 4
-X_CHUNKS = ((0, 512, 192), (512, 256, 96), (768, 256, 64))
+LOADS = ((0, 512), (512, 384), (896, 128))
+BLOCKS = ((0, 0, 512, 192), (1, 512, 256, 0), (1, 768, 128, 128), (2, 896, 128, 48))
+ORDER = (("S", 0), ("V", 0), ("Q", 0), ("M", 0), ("S", 2), ("V", 1), ("Q", 2), ("M", 2), ("S", 3), ("V", 3), ("R", 0), ("Q", 1), ("M", 1), ("Q", 3), ("M", 3), ("R", 2), ("R", 1), ("R", 3))
+TAIL = 384
 
 FLOPS = 2 * K * T * N + 2 * T * N + 2 * D * N * V
 
@@ -29,7 +32,7 @@ def tile_picked_agg_lin_relu_sub_l_kernel(tc, xT, w, b, gate, pos1, pos2, pos3, 
         x_rows = xT.rearrange("(p j) t -> p j t", j=J)
 
         w_raw = [keep.tile([P, J, P], F32, name=f"w_raw{h}") for h in range(2)]
-        x_raw = [keep.tile([P, J, n], F32, name=f"x_raw{c}") for c, (t0, n, s) in enumerate(X_CHUNKS)]
+        x_raw = [keep.tile([P, J, n], F32, name=f"x_raw{c}") for c, (t0, n) in enumerate(LOADS)]
         bias = [keep.tile([P, 1], F32, name=f"bias{h}") for h in range(2)]
         lists = [keep.tile([P, V // 16], U16, name=f"list{d}") for d in range(D)]
         gates = [[keep.tile([P, V], F32, name=f"gate{d}_{h}") for d in range(D)] for h in range(2)]
@@ -40,38 +43,41 @@ def tile_picked_agg_lin_relu_sub_l_kernel(tc, xT, w, b, gate, pos1, pos2, pos3, 
         nc.scalar.activation(warmed[:], warm[:], RELU)
 
         nc.sync.dma_start(out=w_raw[0][:], in_=w_rows[:, :, 0:P])
-        for c, (t0, n, s) in enumerate(X_CHUNKS):
+        for c, (t0, n) in enumerate(LOADS):
             nc.sync.dma_start(out=x_raw[c][:], in_=x_rows[:, :, t0 : t0 + n])
-        for h in range(2):
-            nc.scalar.dma_start(out=bias[h][:], in_=b[h * P : (h + 1) * P, :])
+        nc.scalar.dma_start(out=bias[0][:], in_=b[0:P, :])
         pos = (pos1, pos2, pos3, pos4)
-        nc.sync.dma_start(lists[0][:], pos[0])
-        nc.sync.dma_start(out=gates[0][0][:], in_=gate[0, 0:P, :])
         nc.sync.dma_start(out=w_raw[1][:], in_=w_rows[:, :, P : 2 * P])
-        for d in range(1, D):
+        for d in range(D):
             nc.sync.dma_start(lists[d][:], pos[d])
             nc.sync.dma_start(out=gates[0][d][:], in_=gate[d, 0:P, :])
+            if d == 0:
+                nc.sync.dma_start(out=bias[1][:], in_=b[P : 2 * P, :])
         for d in range(D):
             nc.sync.dma_start(out=gates[1][d][:], in_=gate[d, P : 2 * P, :])
 
         w_grp = [keep.tile([P, P, J], BF16, name=f"w_grp{h}", align_bytes=64) for h in range(2)]
         w_codes = [keep.tile([P, P], U32, name=f"w_codes{h}", align_bytes=64) for h in range(2)]
         w_scales = [keep.tile([P, P], U8, name=f"w_scales{h}", align_bytes=64) for h in range(2)]
-        x_grp = [keep.tile([P, n, J], BF16, name=f"x_grp{c}", align_bytes=64) for c, (t0, n, s) in enumerate(X_CHUNKS)]
-        x_codes = [keep.tile([P, n], U32, name=f"x_codes{c}", align_bytes=64) for c, (t0, n, s) in enumerate(X_CHUNKS)]
-        x_scales = [keep.tile([P, n], U8, name=f"x_scales{c}", align_bytes=64) for c, (t0, n, s) in enumerate(X_CHUNKS)]
+        x_grp = [keep.tile([P, n, J], BF16, name=f"x_grp{c}", align_bytes=64) for c, (l, t0, n, s) in enumerate(BLOCKS)]
+        x_codes = [keep.tile([P, n], U32, name=f"x_codes{c}", align_bytes=64) for c, (l, t0, n, s) in enumerate(BLOCKS)]
+        x_scales = [keep.tile([P, n], U8, name=f"x_scales{c}", align_bytes=64) for c, (l, t0, n, s) in enumerate(BLOCKS)]
         y = [keep.tile([P, T], F32, name=f"y{h}") for h in range(2)]
+
+        def interleave(copy, grouped, raw):
+            copy(
+                out=grouped.rearrange("p (c i) j -> p c j i", i=4),
+                in_=raw.rearrange("p j (c i) -> p c j i", i=4),
+            )
 
         def quantise(codes, scales, grp):
             nc.vector.quantize_mx(
                 out=codes[:].bitcast(FP8X4), scales=scales[:], in_=grp[:].rearrange("p w j -> p (w j)")
             )
 
-        def project(h, c):
-            t0, n, s = X_CHUNKS[c]
-            acc = psum.tile([P, n], F32, name=f"acc{h}_{c}")
+        def project(h, c, acc):
             nc.tensor.matmul_mx(
-                out=acc[:],
+                out=acc,
                 lhsT=w_codes[h][:].bitcast(FP8X4),
                 lhsT_scale=w_scales[h][:],
                 rhs=x_codes[c][:].bitcast(FP8X4),
@@ -79,23 +85,40 @@ def tile_picked_agg_lin_relu_sub_l_kernel(tc, xT, w, b, gate, pos1, pos2, pos3, 
                 start=True,
                 stop=True,
             )
-            return acc
 
-        def activate(h, c, acc):
-            t0, n, s = X_CHUNKS[c]
-            nc.scalar.activation(y[h][:, t0 : t0 + n], acc[:], RELU, bias=bias[h][:])
+        def cast(c, on_scalar):
+            l, t0, n, s = BLOCKS[c]
+            off = t0 - LOADS[l][0]
+            if on_scalar and s:
+                interleave(nc.scalar.copy, x_grp[c][:, n - s : n, :], x_raw[l][:, :, off + n - s : off + n])
+            if not on_scalar and s < n:
+                interleave(nc.vector.tensor_copy, x_grp[c][:, 0 : n - s, :], x_raw[l][:, :, off : off + n - s])
 
-        nc.vector.tensor_copy(out=w_grp[0][:], in_=w_raw[0][:].rearrange("p j m -> p m j"))
+        interleave(nc.vector.tensor_copy, w_grp[0][:], w_raw[0][:])
         quantise(w_codes[0], w_scales[0], w_grp[0])
-        for c, (t0, n, s) in enumerate(X_CHUNKS):
-            v = n - s
-            nc.scalar.copy(out=x_grp[c][:, v:n, :], in_=x_raw[c][:, :, v:n].rearrange("p j t -> p t j"))
-            nc.vector.tensor_copy(out=x_grp[c][:, 0:v, :], in_=x_raw[c][:, :, 0:v].rearrange("p j t -> p t j"))
-            quantise(x_codes[c], x_scales[c], x_grp[c])
-        for c in range(len(X_CHUNKS)):
-            activate(0, c, project(0, c))
+        acc0 = {}
+        for step, c in ORDER:
+            l, t0, n, s = BLOCKS[c]
+            if step == "S":
+                cast(c, True)
+            elif step == "V":
+                cast(c, False)
+            elif step == "Q":
+                quantise(x_codes[c], x_scales[c], x_grp[c])
+            elif step == "M":
+                acc0[c] = psum.tile([P, n], F32, name=f"acc0_{c}")
+                project(0, c, acc0[c][:])
+            elif step == "R":
+                nc.scalar.activation(y[0][:, t0 : t0 + n], acc0[c][:], RELU, bias=bias[0][:])
 
-        nc.scalar.copy(out=w_grp[1][:], in_=w_raw[1][:].rearrange("p j m -> p m j"))
+        interleave(nc.vector.tensor_copy, w_grp[1][:], w_raw[1][:])
+        quantise(w_codes[1], w_scales[1], w_grp[1])
+        for half in range(2):
+            acc1 = psum.tile([P, V], F32, name=f"acc1_{half}")
+            for c, (l, t0, n, s) in enumerate(BLOCKS):
+                if t0 // V == half:
+                    project(1, c, acc1[:, t0 % V : t0 % V + n])
+            nc.scalar.activation(y[1][:, half * V : (half + 1) * V], acc1[:], RELU, bias=bias[1][:])
 
         def fetch(h, d, v0, v1, product):
             nc.vector.tensor_tensor(
@@ -110,9 +133,6 @@ def tile_picked_agg_lin_relu_sub_l_kernel(tc, xT, w, b, gate, pos1, pos2, pos3, 
         total = [keep.tile([P, V], F32, name=f"total{h}") for h in range(2)]
 
         fetch(0, 0, 0, V, pair[0][:, 0, :])
-        quantise(w_codes[1], w_scales[1], w_grp[1])
-        for c in range(len(X_CHUNKS)):
-            activate(1, c, project(1, c))
         fetch(0, 1, 0, V, pair[0][:, 1, :])
         fetch(0, 2, 0, V, pair[1][:, 0, :])
         fetch(0, 3, 0, V, pair[1][:, 1, :])
@@ -123,10 +143,9 @@ def tile_picked_agg_lin_relu_sub_l_kernel(tc, xT, w, b, gate, pos1, pos2, pos3, 
         nc.sync.dma_start(out=out[0:P, :], in_=total[0][:])
         fetch(1, 2, 0, V, prod[2][:])
         nc.vector.tensor_add(s01[:], prod[0][:], prod[1][:])
-        fetch(1, 3, 0, V // 2, prod[3][:, 0 : V // 2])
+        fetch(1, 3, 0, TAIL, prod[3][:, 0:TAIL])
         nc.vector.tensor_add(s012[:], s01[:], prod[2][:])
-        fetch(1, 3, V // 2, V, prod[3][:, V // 2 : V])
-        for v0 in (0, V // 2):
-            cols = slice(v0, v0 + V // 2)
+        fetch(1, 3, TAIL, V, prod[3][:, TAIL:V])
+        for cols in (slice(0, TAIL), slice(TAIL, V)):
             nc.vector.tensor_add(total[1][:, cols], s012[:, cols], prod[3][:, cols])
             nc.sync.dma_start(out=out[P : 2 * P, cols], in_=total[1][:, cols])

from contextlib import ExitStack

import concourse.mybir as mybir

K, T, D, V, N = 512, 1024, 4, 512, 256
P = 128
J = 4
LOADS = ((0, 512), (512, 384), (896, 128))
BLOCKS = ((0, 0, 512, 192), (1, 512, 256, 0), (1, 768, 128, 128), (2, 896, 128, 48))
ORDER = (("S", 0), ("V", 0), ("Q", 0), ("M", 0), ("S", 2), ("V", 1), ("Q", 2), ("M", 2), ("S", 3), ("V", 3), ("R", 0), ("Q", 1), ("M", 1), ("Q", 3), ("M", 3), ("R", 2), ("R", 1), ("R", 3))
TAIL = 384

FLOPS = 2 * K * T * N + 2 * T * N + 2 * D * N * V

F32 = mybir.dt.float32
BF16 = mybir.dt.bfloat16
U32 = mybir.dt.uint32
U16 = mybir.dt.uint16
U8 = mybir.dt.uint8
FP8X4 = mybir.dt.float8_e4m3fn_x4
RELU = mybir.ActivationFunctionType.Relu
MULT = mybir.AluOpType.mult


def tile_picked_agg_lin_relu_sub_l_kernel(tc, xT, w, b, gate, pos1, pos2, pos3, pos4, out):
    nc = tc.nc
    with ExitStack() as ctx:
        keep = ctx.enter_context(tc.tile_pool(name="keep", bufs=1))
        psum = ctx.enter_context(tc.psum_pool(name="psum", bufs=1))

        w_rows = w.rearrange("(p j) m -> p j m", j=J)
        x_rows = xT.rearrange("(p j) t -> p j t", j=J)

        w_raw = [keep.tile([P, J, P], F32, name=f"w_raw{h}") for h in range(2)]
        x_raw = [keep.tile([P, J, n], F32, name=f"x_raw{c}") for c, (t0, n) in enumerate(LOADS)]
        bias = [keep.tile([P, 1], F32, name=f"bias{h}") for h in range(2)]
        lists = [keep.tile([P, V // 16], U16, name=f"list{d}") for d in range(D)]
        gates = [[keep.tile([P, V], F32, name=f"gate{d}_{h}") for d in range(D)] for h in range(2)]

        warm = keep.tile([P, 1], F32, name="warm")
        warmed = keep.tile([P, 1], F32, name="warmed")
        nc.gpsimd.memset(warm[:], 0.0)
        nc.scalar.activation(warmed[:], warm[:], RELU)

        nc.sync.dma_start(out=w_raw[0][:], in_=w_rows[:, :, 0:P])
        for c, (t0, n) in enumerate(LOADS):
            nc.sync.dma_start(out=x_raw[c][:], in_=x_rows[:, :, t0 : t0 + n])
        nc.scalar.dma_start(out=bias[0][:], in_=b[0:P, :])
        pos = (pos1, pos2, pos3, pos4)
        nc.sync.dma_start(out=w_raw[1][:], in_=w_rows[:, :, P : 2 * P])
        for d in range(D):
            nc.sync.dma_start(lists[d][:], pos[d])
            nc.sync.dma_start(out=gates[0][d][:], in_=gate[d, 0:P, :])
            if d == 0:
                nc.sync.dma_start(out=bias[1][:], in_=b[P : 2 * P, :])
        for d in range(D):
            nc.sync.dma_start(out=gates[1][d][:], in_=gate[d, P : 2 * P, :])

        w_grp = [keep.tile([P, P, J], BF16, name=f"w_grp{h}", align_bytes=64) for h in range(2)]
        w_codes = [keep.tile([P, P], U32, name=f"w_codes{h}", align_bytes=64) for h in range(2)]
        w_scales = [keep.tile([P, P], U8, name=f"w_scales{h}", align_bytes=64) for h in range(2)]
        x_grp = [keep.tile([P, n, J], BF16, name=f"x_grp{c}", align_bytes=64) for c, (l, t0, n, s) in enumerate(BLOCKS)]
        x_codes = [keep.tile([P, n], U32, name=f"x_codes{c}", align_bytes=64) for c, (l, t0, n, s) in enumerate(BLOCKS)]
        x_scales = [keep.tile([P, n], U8, name=f"x_scales{c}", align_bytes=64) for c, (l, t0, n, s) in enumerate(BLOCKS)]
        y = [keep.tile([P, T], F32, name=f"y{h}") for h in range(2)]

        def interleave(copy, grouped, raw):
            copy(
                out=grouped.rearrange("p (c i) j -> p c j i", i=4),
                in_=raw.rearrange("p j (c i) -> p c j i", i=4),
            )

        def quantise(codes, scales, grp):
            nc.vector.quantize_mx(
                out=codes[:].bitcast(FP8X4), scales=scales[:], in_=grp[:].rearrange("p w j -> p (w j)")
            )

        def project(h, c, acc):
            nc.tensor.matmul_mx(
                out=acc,
                lhsT=w_codes[h][:].bitcast(FP8X4),
                lhsT_scale=w_scales[h][:],
                rhs=x_codes[c][:].bitcast(FP8X4),
                rhs_scale=x_scales[c][:],
                start=True,
                stop=True,
            )

        def cast(c, on_scalar):
            l, t0, n, s = BLOCKS[c]
            off = t0 - LOADS[l][0]
            if on_scalar and s:
                interleave(nc.scalar.copy, x_grp[c][:, n - s : n, :], x_raw[l][:, :, off + n - s : off + n])
            if not on_scalar and s < n:
                interleave(nc.vector.tensor_copy, x_grp[c][:, 0 : n - s, :], x_raw[l][:, :, off : off + n - s])

        interleave(nc.vector.tensor_copy, w_grp[0][:], w_raw[0][:])
        quantise(w_codes[0], w_scales[0], w_grp[0])
        acc0 = {}
        for step, c in ORDER:
            l, t0, n, s = BLOCKS[c]
            if step == "S":
                cast(c, True)
            elif step == "V":
                cast(c, False)
            elif step == "Q":
                quantise(x_codes[c], x_scales[c], x_grp[c])
            elif step == "M":
                acc0[c] = psum.tile([P, n], F32, name=f"acc0_{c}")
                project(0, c, acc0[c][:])
            elif step == "R":
                nc.scalar.activation(y[0][:, t0 : t0 + n], acc0[c][:], RELU, bias=bias[0][:])

        interleave(nc.vector.tensor_copy, w_grp[1][:], w_raw[1][:])
        quantise(w_codes[1], w_scales[1], w_grp[1])
        for half in range(2):
            acc1 = psum.tile([P, V], F32, name=f"acc1_{half}")
            for c, (l, t0, n, s) in enumerate(BLOCKS):
                if t0 // V == half:
                    project(1, c, acc1[:, t0 % V : t0 % V + n])
            nc.scalar.activation(y[1][:, half * V : (half + 1) * V], acc1[:], RELU, bias=bias[1][:])

        def fetch(h, d, v0, v1, product):
            nc.vector.tensor_tensor(
                product, y[h][:].indirect(lists[d][:, v0 // 16 : v1 // 16]), gates[h][d][:, v0:v1], MULT
            )

        pair = [keep.tile([P, 2, V], F32, name=f"pair{d}") for d in (0, 2)]
        pair_sum = keep.tile([P, 2, V], F32, name="pair_sum")
        prod = [keep.tile([P, V], F32, name=f"prod{d}") for d in range(D)]
        s01 = keep.tile([P, V], F32, name="s01")
        s012 = keep.tile([P, V], F32, name="s012")
        total = [keep.tile([P, V], F32, name=f"total{h}") for h in range(2)]

        fetch(0, 0, 0, V, pair[0][:, 0, :])
        fetch(0, 1, 0, V, pair[0][:, 1, :])
        fetch(0, 2, 0, V, pair[1][:, 0, :])
        fetch(0, 3, 0, V, pair[1][:, 1, :])
        fetch(1, 0, 0, V, prod[0][:])
        nc.vector.tensor_add(pair_sum[:], pair[0][:], pair[1][:])
        fetch(1, 1, 0, V, prod[1][:])
        nc.vector.tensor_add(total[0][:], pair_sum[:, 0, :], pair_sum[:, 1, :])
        nc.sync.dma_start(out=out[0:P, :], in_=total[0][:])
        fetch(1, 2, 0, V, prod[2][:])
        nc.vector.tensor_add(s01[:], prod[0][:], prod[1][:])
        fetch(1, 3, 0, TAIL, prod[3][:, 0:TAIL])
        nc.vector.tensor_add(s012[:], s01[:], prod[2][:])
        fetch(1, 3, TAIL, V, prod[3][:, TAIL:V])
        for cols in (slice(0, TAIL), slice(TAIL, V)):
            nc.vector.tensor_add(total[1][:, cols], s012[:, cols], prod[3][:, cols])
            nc.sync.dma_start(out=out[P : 2 * P, cols], in_=total[1][:, cols])
